import numpy as np
import ml_dtypes


def mxq(x, axis, fmt="e4m3"):
    dtype, down = {"e4m3": (ml_dtypes.float8_e4m3fn, 7), "e5m2": (ml_dtypes.float8_e5m2, 14)}[fmt]
    v = np.moveaxis(np.asarray(x, np.float32).astype(ml_dtypes.bfloat16).astype(np.float64), axis, -1)
    blocks = v.reshape(v.shape[:-1] + (-1, 32))
    amax = np.abs(blocks).max(-1, keepdims=True)
    byte = np.maximum(np.where(amax > 0, np.frexp(amax)[1] - 1 + 127, 0) - down, 1)
    scale = np.exp2(byte - 127.0)
    codes = (blocks / scale).astype(np.float32).astype(dtype).astype(np.float64)
    return np.moveaxis((codes * scale).reshape(v.shape), -1, axis)


WIDE = False


def mx_kscale(k):
    if not WIDE:
        return np.ones(k)
    levels = np.array([10, -10, 5, -5, 0])
    if k % 512:
        return np.exp2(np.random.permutation(np.resize(levels, k // 32))).repeat(32)
    a = np.empty((k // 512, 16))
    for p in range(k // 512):
        a[p, :8] = np.random.permutation(np.resize(levels, 8))
        for g in range(8):
            far = levels[np.abs(levels - a[p, g]) >= 10]
            a[p, g + 8] = far[np.random.randint(len(far))]
    return np.exp2(a.ravel()).repeat(32)


def f64(x):
    return np.asarray(x).astype(np.float64)


def striped(idx):
    return np.tile(idx.reshape(-1, 16).T, (8, 1)).astype(np.uint16)


def unstriped(offs):
    return offs[:16].T.reshape(-1).astype(np.int64)


def striped8(idx):
    return np.concatenate([x.reshape(-1, 16).T for x in idx]).astype(np.uint16)


def runs(offs, k):
    lists = np.stack([offs[16 * r : 16 * r + 16].T.reshape(-1) for r in range(8)]).astype(np.int64)
    return lists[np.arange(k) % 512 // 64]


def pack_weight(w):
    k, n = w.shape
    w = f64(np.asarray(w, np.float32).astype(ml_dtypes.bfloat16)).reshape(k // 32, 32, n)
    amax = np.abs(w).max(1)
    byte = np.clip(np.where(amax > 0, np.frexp(amax)[1] - 1 + 127 - 7, 1), 1, 254)
    scaled = (w * np.exp2(127.0 - byte)[:, None, :]).reshape(k, n).astype(np.float32)
    words = np.ascontiguousarray(scaled.reshape(k // 512, 128, 4, n).transpose(0, 1, 3, 2)).astype(ml_dtypes.float8_e4m3fn).view(np.uint8)
    return words, np.ascontiguousarray(byte.astype(np.uint8).reshape(k // 512, 16, n))


def unpack_weight(words, scales):
    g, p, n, _ = words.shape
    vals = np.ascontiguousarray(words).view(ml_dtypes.float8_e4m3fn).astype(np.float64) * np.repeat(np.exp2(scales.astype(np.float64) - 127.0), 8, axis=1)[..., None]
    return vals.transpose(0, 1, 3, 2).reshape(g * 512, n)


def sigmoid(v):
    return 1.0 / (1.0 + np.exp(-np.maximum(v, -700.0)))

def planes(y):
    n, m = y.shape
    v = y.astype(np.float32).astype(ml_dtypes.bfloat16).astype(np.float64).reshape(n // 32, 32, m)
    top = np.abs(v).max(1)
    byte = np.clip(np.where(top > 0, np.frexp(top)[1] - 1 + 127 - 7, 1), 1, 254)
    codes = (v * np.exp2(127.0 - byte)[:, None, :]).reshape(n, m).astype(np.float32).astype(ml_dtypes.float8_e4m3fn).view(np.uint8)
    words = codes.reshape(n // 512, 128, 4, m).transpose(0, 1, 3, 2)
    return np.ascontiguousarray(words), np.ascontiguousarray(byte.astype(np.uint8).reshape(n // 512, 16, m))


K, T, S, G, H, U = 512, 1024, 512, 2048, 512, 1024


def setup_inputs():
    n = np.random.standard_normal
    s = mx_kscale(K)[:, None]
    packed_xT = pack_weight(n((K, T)) * s)
    packed_dT = pack_weight(n((K, G)) / s)
    return {
        "x_words": packed_xT[0],
        "x_scales": packed_xT[1],
        "d_words": packed_dT[0],
        "d_scales": packed_dT[1],
        "gs": (np.random.uniform(0.5, 1.5, (K, 1)) * s).astype(np.float32),
        "mem": n((H, U)).astype(np.float32),
        "offs": striped(np.random.permutation(T)[:S]),
        "k1": striped8(np.random.randint(0, G, (8, H))),
        "n1": striped8(np.stack([np.random.permutation(S) for _ in range(8)])),
        "k2": striped8(np.random.randint(0, G, (8, H))),
        "n2": striped8(np.stack([np.random.permutation(U)[:S] for _ in range(8)])),
    }


def reference(x_words, x_scales, d_words, d_scales, gs, mem, offs, k1, n1, k2, n2):
    d_k2 = unpack_weight(d_words, d_scales)[np.arange(K)[:, None], runs(k2, K)]
    d_k1 = unpack_weight(d_words, d_scales)[np.arange(K)[:, None], runs(k1, K)]
    xq = unpack_weight(x_words, x_scales)[:, unstriped(offs)]
    h = 0.0625 * (d_k1.T @ xq)
    z = f64(gs) * (h * (sigmoid(h[np.arange(H)[:, None], runs(n1, H)])))
    h2 = 0.0625 * ((d_k2.T @ mxq(z, 0, "e4m3")))
    out = f64(mem).copy()
    out[np.arange(H)[:, None], runs(n2, H)] = h2
    return (out,) + planes(out)

@@ -1,0 +1,231 @@
+from contextlib import ExitStack
+
+import concourse.mybir as mybir
+
+F32 = mybir.dt.float32
+BF16 = mybir.dt.bfloat16
+I32 = mybir.dt.int32
+U32 = mybir.dt.uint32
+U16 = mybir.dt.uint16
+U8 = mybir.dt.uint8
+FP8X4 = mybir.dt.float8_e4m3fn_x4
+ACT = mybir.ActivationFunctionType
+MULT = mybir.AluOpType.mult
+ADD = mybir.AluOpType.add
+
+P = 128
+PACK = 4
+T, S, G, H, U = 1024, 512, 2048, 512, 1024
+K = 512
+CHUNK = 128
+VECTOR_GATHER_CHUNKS = 4
+FLOPS = 2 * 2 * K * H * S
+
+
+def tile_picked_codegatepage_none_po_kernel(
+    tc, x_words, x_scales, d_words, d_scales, gs, mem, offs, k1, n1, k2, n2, out_0, out_1, out_2
+):
+    nc = tc.nc
+    with ExitStack() as ctx:
+        lists = ctx.enter_context(tc.tile_pool(name="lists", bufs=1))
+        keep = ctx.enter_context(tc.tile_pool(name="keep", bufs=1))
+        pages = ctx.enter_context(tc.tile_pool(name="pages", bufs=1))
+        psum = ctx.enter_context(tc.psum_pool(name="psum", bufs=1))
+
+        def load_list(name, source):
+            tile = lists.tile([P, S // 16], U16, name=name)
+            nc.sync.dma_start(tile[:], source)
+            return tile
+
+        def load_scale_rows(name, source, width):
+            tile = keep.tile([P, width], U8, name=name, align_bytes=64)
+            rows = source[0].bitcast(I32).unsqueeze(1).to_broadcast([16, 8, width // 4])
+            nc.sync.dma_start(tile[:].bitcast(I32), rows)
+            return tile
+
+        def load_words(name, source, width):
+            tile = keep.tile([P, width], U32, name=name, align_bytes=64)
+            nc.sync.dma_start(tile[:].bitcast(I32), source[0].rearrange("p c r -> p (c r)").bitcast(I32))
+            return tile
+
+        offs_list = load_list("offs_list", offs)
+        x_scale_table = load_scale_rows("x_scale_table", x_scales, T)
+        k1_list = load_list("k1_list", k1)
+        d_scale_table = load_scale_rows("d_scale_table", d_scales, G)
+        d_word_table = load_words("d_word_table", d_words, G)
+        x_word_table = load_words("x_word_table", x_words, T)
+        k2_list = load_list("k2_list", k2)
+        n1_list = load_list("n1_list", n1)
+        gains = keep.tile([P, PACK], F32, name="gains")
+        nc.gpsimd.dma_start(gains[:], gs.rearrange("(p t) o -> p (t o)", t=PACK))
+        n2_list = load_list("n2_list", n2)
+
+        plane_1 = keep.tile([P, H + S], U8, name="plane_1", align_bytes=64)
+        plane_2 = keep.tile([P, H], U8, name="plane_2", align_bytes=64)
+        nc.gpsimd.memset(plane_1[:].bitcast(I32), 0)
+        nc.gpsimd.memset(plane_2[:].bitcast(I32), 0)
+
+        def gather(name, table, index_list, dtype):
+            tile = keep.tile([P, S], dtype, name=name, align_bytes=64)
+            nc.vector.tensor_copy(tile[:], table[:].indirect(index_list[:]))
+            return tile
+
+        def deal(dealt, picked, run):
+            nc.vector.tensor_copy(
+                dealt.rearrange("p (t b i) -> p b t i", t=PACK, i=run),
+                picked.rearrange("p (b i t) -> p b t i", t=PACK, i=run),
+            )
+
+        def place_scale_rows(plane, staged):
+            for q in range(4):
+                nc.sync.dma_start(
+                    plane[32 * q : 32 * q + 4, :].bitcast(I32),
+                    staged[32 * q : 32 * q + 32 : 8, :].bitcast(I32),
+                )
+
+        page_bytes = 4 * U
+        staged_1 = pages.tile([P, H + S], U8, name="staged_1", offset=page_bytes - 512)
+        staged_2 = pages.tile([P, H], U8, name="staged_2", offset=3 * page_bytes - 256)
+
+        x_picked_scales = gather("x_picked_scales", x_scale_table, offs_list, U8)
+        k1_scales = gather("k1_scales", d_scale_table, k1_list, U8)
+        nc.vector.tensor_copy(staged_1[:, H : H + S].bitcast(I32), x_picked_scales[:].bitcast(I32))
+        deal(staged_1[:, 0:H], k1_scales[:], 16)
+        place_scale_rows(plane_1, staged_1)
+        k1_words = gather("k1_words", d_word_table, k1_list, U32)
+        x_picked = gather("x_picked", x_word_table, offs_list, U32)
+        w1 = keep.tile([P, H], U32, name="w1", align_bytes=64)
+        deal(w1[:].bitcast(I32), k1_words[:].bitcast(I32), 4)
+
+        gains_16 = keep.tile([P, PACK], F32, name="gains_16")
+        nc.gpsimd.tensor_scalar(gains_16[:], gains[:], 0.0625, 0.0, MULT, ADD)
+
+        h_banks = [psum.tile([P, S], F32, name=f"h_bank{t}") for t in range(PACK)]
+        for t in range(PACK):
+            rows = slice(P * t, P * (t + 1))
+            nc.tensor.matmul_mx(
+                out=h_banks[t][:],
+                lhsT=w1[:, rows].bitcast(FP8X4),
+                lhsT_scale=plane_1[:, rows],
+                rhs=x_picked[:].bitcast(FP8X4),
+                rhs_scale=plane_1[:, H : H + S],
+                start=True,
+                stop=True,
+            )
+
+        k2_scales = gather("k2_scales", d_scale_table, k2_list, U8)
+        deal(staged_2[:], k2_scales[:], 16)
+        place_scale_rows(plane_2, staged_2)
+        k2_words = gather("k2_words", d_word_table, k2_list, U32)
+        w2 = keep.tile([P, H], U32, name="w2", align_bytes=64)
+        deal(w2[:].bitcast(I32), k2_words[:].bitcast(I32), 4)
+
+        page = [pages.tile([P, U], F32, name=f"page{t}", offset=page_bytes * t) for t in range(PACK)]
+        mem_rows = mem.rearrange("(p t) w -> p t w", t=PACK)
+        out_rows = out_0.rearrange("(p t) w -> p t w", t=PACK)
+        for t in range(PACK):
+            nc.sync.dma_start(page[t][:], mem_rows[:, t, :])
+
+        sig_rows = [keep.tile([P, S], F32, name=f"sig_rows{t}") for t in range(PACK)]
+        h2_late = keep.tile([P, 2, S], F32, name="h2_late")
+        chunks = S // CHUNK
+        gained_late = keep.tile([P, PACK, 2 * CHUNK], F32, name="gained_late")
+
+        def scatter(t, start, source):
+            width = source.shape[1]
+            nc.vector.tensor_copy(page[t][:].indirect(n2_list[:, start // 16 : (start + width) // 16]), source)
+
+        def second_layer(c):
+            cols = slice(c * CHUNK, (c + 1) * CHUNK)
+            gates = keep.tile([P, PACK, CHUNK], F32, name=f"gates{c}", tag=f"gates{c}", align_bytes=64)
+            if c < 2:
+                gained = keep.tile([P, PACK, CHUNK], F32, name=f"gained{c}")[:]
+            else:
+                gained = gained_late[:, :, (c - 2) * CHUNK : (c - 1) * CHUNK]
+            offsets = n1_list[:, c * CHUNK // 16 : (c + 1) * CHUNK // 16]
+            for t in range(PACK):
+                if c == 0:
+                    nc.scalar.activation(sig_rows[t][:], h_banks[t][:], ACT.Sigmoid, scale=0.0625)
+                if t == PACK - 1 and c < VECTOR_GATHER_CHUNKS:
+                    nc.vector.tensor_copy(gates[:, t, :], sig_rows[t][:].indirect(offsets))
+                else:
+                    nc.scalar.activation(gates[:, t, :], sig_rows[t][:].indirect(offsets), ACT.Copy)
+                if c < 2:
+                    nc.vector.tensor_scalar(gained[:, t, :], h_banks[t][:, cols], gains_16[:, t : t + 1], None, MULT)
+                elif c == 2:
+                    nc.scalar.activation(gained_late[:, t, :], h_banks[t][:, 2 * CHUNK : S], ACT.Copy, scale=gains_16[:, t : t + 1])
+            z = keep.tile([P, CHUNK * PACK], BF16, name=f"z{c}", tag=f"z{c}", align_bytes=64)
+            nc.vector.tensor_tensor(
+                z[:].rearrange("p (b i t) -> p b t i", t=PACK, i=4),
+                gained.rearrange("p t (b i) -> p b t i", i=4),
+                gates[:].rearrange("p t (b i) -> p b t i", i=4),
+                MULT,
+            )
+            z_words = keep.tile([P, CHUNK], U32, name=f"z_words{c}", align_bytes=64)
+            z_scales = keep.tile([P, CHUNK], U8, name=f"z_scales{c}", align_bytes=64)
+            nc.vector.quantize_mx(out=z_words[:].bitcast(FP8X4), scales=z_scales[:], in_=z[:])
+            h2_bank = psum.tile([P, PACK, CHUNK], F32, name=f"h2_bank{c}")
+            for t in range(PACK):
+                rows = slice(P * t, P * (t + 1))
+                nc.tensor.matmul_mx(
+                    out=h2_bank[:, t, :],
+                    lhsT=w2[:, rows].bitcast(FP8X4),
+                    lhsT_scale=plane_2[:, rows],
+                    rhs=z_words[:].bitcast(FP8X4),
+                    rhs_scale=z_scales[:],
+                    start=True,
+                    stop=True,
+                )
+            return h2_bank
+
+        bank = second_layer(0)
+        for c in range(chunks):
+            cols = slice(c * CHUNK, (c + 1) * CHUNK)
+            h2_0 = keep.tile([P, CHUNK], F32, name=f"h2_0_{c}", tag=f"z{c + 1}", align_bytes=64)
+            if c == 0:
+                nc.vector.tensor_scalar(h2_0[:], bank[:, 0, :], 0.0625, None, MULT)
+            else:
+                nc.scalar.activation(h2_0[:], bank[:, 0, :], ACT.Copy, scale=0.0625)
+            nc.scalar.activation(h2_late[:, :, cols], bank[:, 2:PACK, :], ACT.Copy, scale=0.0625)
+            scatter(0, c * CHUNK, h2_0[:])
+            next_bank = second_layer(c + 1) if c + 1 < chunks else None
+            h2_1 = keep.tile([P, CHUNK], F32, name=f"h2_1_{c}", tag=f"gates{c + 1}", align_bytes=64)
+            nc.scalar.activation(h2_1[:], bank[:, 1, :], ACT.Copy, scale=0.0625)
+            scatter(1, c * CHUNK, h2_1[:])
+            if c < 2:
+                scatter(2, c * CHUNK, h2_late[:, 0, cols])
+            bank = next_bank
+        scatter(2, 2 * CHUNK, h2_late[:, 0, 2 * CHUNK : S])
+        scatter(3, 0, h2_late[:, 1, :])
+
+        for t in range(PACK):
+            nc.sync.dma_start(out_rows[:, t, :], page[t][:])
+
+        split = 384
+        rounded = keep.tile([P, PACK, U], BF16, name="rounded")
+        for t in range(PACK - 1):
+            nc.scalar.copy(rounded[:, t, :], page[t][:])
+        pieces = [(0, split), (split, 640), (640, 896), (896, U)]
+        grouped = [keep.tile([P, (b - a) * PACK], BF16, name=f"grouped{a}", align_bytes=64) for a, b in pieces]
+        for (a, b), tile in list(zip(pieces, grouped))[1:]:
+            nc.scalar.copy(
+                tile[:].rearrange("p (b i t) -> p b t i", t=PACK, i=4)[:, :, 0 : PACK - 1, :],
+                rounded[:, 0 : PACK - 1, a:b].rearrange("p t (b i) -> p b t i", i=4),
+            )
+        for (a, b), tile in list(zip(pieces, grouped))[1:]:
+            nc.scalar.copy(tile[:].rearrange("p (c t) -> p c t", t=PACK)[:, :, PACK - 1], page[PACK - 1][:, a:b])
+        nc.vector.tensor_copy(rounded[:, PACK - 1, 0:split], page[PACK - 1][:, 0:split])
+        nc.vector.tensor_copy(
+            grouped[0][:].rearrange("p (b i t) -> p b t i", t=PACK, i=4),
+            rounded[:, :, 0:split].rearrange("p t (b i) -> p b t i", i=4),
+        )
+        out_words = keep.tile([P, U], U32, name="out_words", align_bytes=64)
+        out_scales = keep.tile([P, U], U8, name="out_scales", align_bytes=64)
+        words_hbm = out_1[0].rearrange("p c r -> p (c r)").bitcast(I32)
+        scales_hbm = out_2[0].bitcast(I32)
+        for (a, b), tile in zip(pieces, grouped):
+            nc.vector.quantize_mx(out=out_words[:, a:b].bitcast(FP8X4), scales=out_scales[:, a:b], in_=tile[:])
+            nc.sync.dma_start(words_hbm[:, a:b], out_words[:, a:b].bitcast(I32))
+        for q in range(4):
+            queue = nc.scalar if q % 2 else nc.sync
+            queue.dma_start(scales_hbm[4 * q : 4 * q + 4, :], out_scales[32 * q : 32 * q + 4, :].bitcast(I32))

@@ -17,8 +17,8 @@ P = 128
 PACK = 4
 T, S, G, H, U = 1024, 512, 2048, 512, 1024
 K = 512
-CHUNK = 128
-VECTOR_GATHER_CHUNKS = 4
+CHUNK = 256
+SCALAR_GATHERS = (0, 2)
 FLOPS = 2 * 2 * K * H * S
 
 
@@ -127,76 +127,56 @@ def tile_picked_codegatepage_none_po_kernel(
             nc.sync.dma_start(page[t][:], mem_rows[:, t, :])
 
         sig_rows = [keep.tile([P, S], F32, name=f"sig_rows{t}") for t in range(PACK)]
-        h2_late = keep.tile([P, 2, S], F32, name="h2_late")
-        chunks = S // CHUNK
-        gained_late = keep.tile([P, PACK, 2 * CHUNK], F32, name="gained_late")
+        gained = keep.tile([P, PACK, S], F32, name="gained")
+        for t in range(PACK):
+            nc.scalar.activation(sig_rows[t][:], h_banks[t][:], ACT.Sigmoid, scale=0.0625)
+        for t in range(PACK):
+            nc.scalar.activation(gained[:, t, :], h_banks[t][:], ACT.Copy, scale=gains_16[:, t : t + 1])
 
-        def scatter(t, start, source):
-            width = source.shape[1]
-            nc.vector.tensor_copy(page[t][:].indirect(n2_list[:, start // 16 : (start + width) // 16]), source)
-
-        def second_layer(c):
+        h2 = keep.tile([P, PACK, S], F32, name="h2")
+        for c in range(S // CHUNK):
             cols = slice(c * CHUNK, (c + 1) * CHUNK)
-            gates = keep.tile([P, PACK, CHUNK], F32, name=f"gates{c}", tag=f"gates{c}", align_bytes=64)
-            if c < 2:
-                gained = keep.tile([P, PACK, CHUNK], F32, name=f"gained{c}")[:]
-            else:
-                gained = gained_late[:, :, (c - 2) * CHUNK : (c - 1) * CHUNK]
+            gates = keep.tile([P, PACK, CHUNK], F32, name=f"gates{c}")
             offsets = n1_list[:, c * CHUNK // 16 : (c + 1) * CHUNK // 16]
             for t in range(PACK):
-                if c == 0:
-                    nc.scalar.activation(sig_rows[t][:], h_banks[t][:], ACT.Sigmoid, scale=0.0625)
-                if t == PACK - 1 and c < VECTOR_GATHER_CHUNKS:
-                    nc.vector.tensor_copy(gates[:, t, :], sig_rows[t][:].indirect(offsets))
-                else:
+                if t < SCALAR_GATHERS[c]:
                     nc.scalar.activation(gates[:, t, :], sig_rows[t][:].indirect(offsets), ACT.Copy)
-                if c < 2:
-                    nc.vector.tensor_scalar(gained[:, t, :], h_banks[t][:, cols], gains_16[:, t : t + 1], None, MULT)
-                elif c == 2:
-                    nc.scalar.activation(gained_late[:, t, :], h_banks[t][:, 2 * CHUNK : S], ACT.Copy, scale=gains_16[:, t : t + 1])
-            z = keep.tile([P, CHUNK * PACK], BF16, name=f"z{c}", tag=f"z{c}", align_bytes=64)
+                else:
+                    nc.vector.tensor_copy(gates[:, t, :], sig_rows[t][:].indirect(offsets))
+            z = keep.tile([P, CHUNK * PACK], BF16, name=f"z{c}", align_bytes=64)
             nc.vector.tensor_tensor(
                 z[:].rearrange("p (b i t) -> p b t i", t=PACK, i=4),
-                gained.rearrange("p t (b i) -> p b t i", i=4),
+                gained[:, :, cols].rearrange("p t (b i) -> p b t i", i=4),
                 gates[:].rearrange("p t (b i) -> p b t i", i=4),
                 MULT,
             )
             z_words = keep.tile([P, CHUNK], U32, name=f"z_words{c}", align_bytes=64)
             z_scales = keep.tile([P, CHUNK], U8, name=f"z_scales{c}", align_bytes=64)
             nc.vector.quantize_mx(out=z_words[:].bitcast(FP8X4), scales=z_scales[:], in_=z[:])
-            h2_bank = psum.tile([P, PACK, CHUNK], F32, name=f"h2_bank{c}")
-            for t in range(PACK):
-                rows = slice(P * t, P * (t + 1))
-                nc.tensor.matmul_mx(
-                    out=h2_bank[:, t, :],
-                    lhsT=w2[:, rows].bitcast(FP8X4),
-                    lhsT_scale=plane_2[:, rows],
-                    rhs=z_words[:].bitcast(FP8X4),
-                    rhs_scale=z_scales[:],
-                    start=True,
-                    stop=True,
-                )
-            return h2_bank
+            for pair in range(2):
+                h2_bank = psum.tile([P, 2, CHUNK], F32, name=f"h2_bank{c}_{pair}")
+                for u in range(2):
+                    t = 2 * pair + u
+                    rows = slice(P * t, P * (t + 1))
+                    nc.tensor.matmul_mx(
+                        out=h2_bank[:, u, :],
+                        lhsT=w2[:, rows].bitcast(FP8X4),
+                        lhsT_scale=plane_2[:, rows],
+                        rhs=z_words[:].bitcast(FP8X4),
+                        rhs_scale=z_scales[:],
+                        start=True,
+                        stop=True,
+                    )
+                nc.scalar.activation(h2[:, 2 * pair : 2 * pair + 2, cols], h2_bank[:], ACT.Copy, scale=0.0625)
 
-        bank = second_layer(0)
-        for c in range(chunks):
-            cols = slice(c * CHUNK, (c + 1) * CHUNK)
-            h2_0 = keep.tile([P, CHUNK], F32, name=f"h2_0_{c}", tag=f"z{c + 1}", align_bytes=64)
-            if c == 0:
-                nc.vector.tensor_scalar(h2_0[:], bank[:, 0, :], 0.0625, None, MULT)
-            else:
-                nc.scalar.activation(h2_0[:], bank[:, 0, :], ACT.Copy, scale=0.0625)
-            nc.scalar.activation(h2_late[:, :, cols], bank[:, 2:PACK, :], ACT.Copy, scale=0.0625)
-            scatter(0, c * CHUNK, h2_0[:])
-            next_bank = second_layer(c + 1) if c + 1 < chunks else None
-            h2_1 = keep.tile([P, CHUNK], F32, name=f"h2_1_{c}", tag=f"gates{c + 1}", align_bytes=64)
-            nc.scalar.activation(h2_1[:], bank[:, 1, :], ACT.Copy, scale=0.0625)
-            scatter(1, c * CHUNK, h2_1[:])
-            if c < 2:
-                scatter(2, c * CHUNK, h2_late[:, 0, cols])
-            bank = next_bank
-        scatter(2, 2 * CHUNK, h2_late[:, 0, 2 * CHUNK : S])
-        scatter(3, 0, h2_late[:, 1, :])
+        def scatter(t, start, stop):
+            nc.vector.tensor_copy(page[t][:].indirect(n2_list[:, start // 16 : stop // 16]), h2[:, t, start:stop])
+
+        for start in (0, CHUNK):
+            for t in range(2):
+                scatter(t, start, start + CHUNK)
+        for t in range(2, PACK):
+            scatter(t, 0, S)
 
         for t in range(PACK):
             nc.sync.dma_start(out_rows[:, t, :], page[t][:])

@@ -30,6 +30,7 @@ def tile_picked_codegatepage_none_po_kernel(
         lists = ctx.enter_context(tc.tile_pool(name="lists", bufs=1))
         keep = ctx.enter_context(tc.tile_pool(name="keep", bufs=1))
         pages = ctx.enter_context(tc.tile_pool(name="pages", bufs=1))
+        picks = ctx.enter_context(tc.tile_pool(name="picks", bufs=1))
         psum = ctx.enter_context(tc.psum_pool(name="psum", bufs=1))
 
         def load_list(name, source):
@@ -65,8 +66,9 @@ def tile_picked_codegatepage_none_po_kernel(
         nc.gpsimd.memset(plane_1[:].bitcast(I32), 0)
         nc.gpsimd.memset(plane_2[:].bitcast(I32), 0)
 
-        def gather(name, table, index_list, dtype):
-            tile = keep.tile([P, S], dtype, name=name, align_bytes=64)
+        def gather(name, table, index_list, dtype, offset=None):
+            pool = keep if offset is None else picks
+            tile = pool.tile([P, S], dtype, name=name, align_bytes=64, offset=offset)
             nc.vector.tensor_copy(tile[:], table[:].indirect(index_list[:]))
             return tile
 
@@ -92,7 +94,7 @@ def tile_picked_codegatepage_none_po_kernel(
         nc.vector.tensor_copy(staged_1[:, H : H + S].bitcast(I32), x_picked_scales[:].bitcast(I32))
         deal(staged_1[:, 0:H], k1_scales[:], 16)
         place_scale_rows(plane_1, staged_1)
-        k1_words = gather("k1_words", d_word_table, k1_list, U32)
+        k1_words = gather("k1_words", d_word_table, k1_list, U32, 0)
         x_picked = gather("x_picked", x_word_table, offs_list, U32)
         w1 = keep.tile([P, H], U32, name="w1", align_bytes=64)
         deal(w1[:].bitcast(I32), k1_words[:].bitcast(I32), 4)
@@ -113,10 +115,10 @@ def tile_picked_codegatepage_none_po_kernel(
                 stop=True,
             )
 
-        k2_scales = gather("k2_scales", d_scale_table, k2_list, U8)
+        k2_scales = gather("k2_scales", d_scale_table, k2_list, U8, 0)
         deal(staged_2[:], k2_scales[:], 16)
         place_scale_rows(plane_2, staged_2)
-        k2_words = gather("k2_words", d_word_table, k2_list, U32)
+        k2_words = gather("k2_words", d_word_table, k2_list, U32, S)
         w2 = keep.tile([P, H], U32, name="w2", align_bytes=64)
         deal(w2[:].bitcast(I32), k2_words[:].bitcast(I32), 4)
 
@@ -127,16 +129,16 @@ def tile_picked_codegatepage_none_po_kernel(
             nc.sync.dma_start(page[t][:], mem_rows[:, t, :])
 
         sig_rows = [keep.tile([P, S], F32, name=f"sig_rows{t}") for t in range(PACK)]
-        gained = keep.tile([P, PACK, S], F32, name="gained")
         for t in range(PACK):
             nc.scalar.activation(sig_rows[t][:], h_banks[t][:], ACT.Sigmoid, scale=0.0625)
-        for t in range(PACK):
-            nc.scalar.activation(gained[:, t, :], h_banks[t][:], ACT.Copy, scale=gains_16[:, t : t + 1])
 
         h2 = keep.tile([P, PACK, S], F32, name="h2")
         for c in range(S // CHUNK):
             cols = slice(c * CHUNK, (c + 1) * CHUNK)
             gates = keep.tile([P, PACK, CHUNK], F32, name=f"gates{c}")
+            gained = keep.tile([P, PACK, CHUNK], F32, name=f"gained{c}")
+            for t in range(PACK):
+                nc.scalar.activation(gained[:, t, :], h_banks[t][:, cols], ACT.Copy, scale=gains_16[:, t : t + 1])
             offsets = n1_list[:, c * CHUNK // 16 : (c + 1) * CHUNK // 16]
             for t in range(PACK):
                 if t < SCALAR_GATHERS[c]:
@@ -146,7 +148,7 @@ def tile_picked_codegatepage_none_po_kernel(
             z = keep.tile([P, CHUNK * PACK], BF16, name=f"z{c}", align_bytes=64)
             nc.vector.tensor_tensor(
                 z[:].rearrange("p (b i t) -> p b t i", t=PACK, i=4),
-                gained[:, :, cols].rearrange("p t (b i) -> p b t i", i=4),
+                gained[:].rearrange("p t (b i) -> p b t i", i=4),
                 gates[:].rearrange("p t (b i) -> p b t i", i=4),
                 MULT,
             )
@@ -183,28 +185,35 @@ def tile_picked_codegatepage_none_po_kernel(
 
         split = 384
         rounded = keep.tile([P, PACK, U], BF16, name="rounded")
-        for t in range(PACK - 1):
+        for t in range(PACK - 2):
             nc.scalar.copy(rounded[:, t, :], page[t][:])
-        pieces = [(0, split), (split, 640), (640, 896), (896, U)]
+        nc.scalar.copy(rounded[:, PACK - 2, split:U], page[PACK - 2][:, split:U])
+        nc.scalar.copy(rounded[:, PACK - 2, 0:split], page[PACK - 2][:, 0:split])
+        vector_pieces = [(0, 128), (128, split)]
+        scalar_pieces = [(split, 640), (640, 896), (896, U)]
+        pieces = vector_pieces + scalar_pieces
         grouped = [keep.tile([P, (b - a) * PACK], BF16, name=f"grouped{a}", align_bytes=64) for a, b in pieces]
-        for (a, b), tile in list(zip(pieces, grouped))[1:]:
+        for (a, b), tile in zip(scalar_pieces, grouped[2:]):
             nc.scalar.copy(
                 tile[:].rearrange("p (b i t) -> p b t i", t=PACK, i=4)[:, :, 0 : PACK - 1, :],
                 rounded[:, 0 : PACK - 1, a:b].rearrange("p t (b i) -> p b t i", i=4),
             )
-        for (a, b), tile in list(zip(pieces, grouped))[1:]:
+        for (a, b), tile in zip(scalar_pieces, grouped[2:]):
             nc.scalar.copy(tile[:].rearrange("p (c t) -> p c t", t=PACK)[:, :, PACK - 1], page[PACK - 1][:, a:b])
-        nc.vector.tensor_copy(rounded[:, PACK - 1, 0:split], page[PACK - 1][:, 0:split])
-        nc.vector.tensor_copy(
-            grouped[0][:].rearrange("p (b i t) -> p b t i", t=PACK, i=4),
-            rounded[:, :, 0:split].rearrange("p t (b i) -> p b t i", i=4),
-        )
+        for a, b in vector_pieces:
+            nc.vector.tensor_copy(rounded[:, PACK - 1, a:b], page[PACK - 1][:, a:b])
+        for (a, b), tile in zip(vector_pieces, grouped):
+            nc.vector.tensor_copy(
+                tile[:].rearrange("p (b i t) -> p b t i", t=PACK, i=4),
+                rounded[:, :, a:b].rearrange("p t (b i) -> p b t i", i=4),
+            )
         out_words = keep.tile([P, U], U32, name="out_words", align_bytes=64)
         out_scales = keep.tile([P, U], U8, name="out_scales", align_bytes=64)
         words_hbm = out_1[0].rearrange("p c r -> p (c r)").bitcast(I32)
         scales_hbm = out_2[0].bitcast(I32)
         for (a, b), tile in zip(pieces, grouped):
             nc.vector.quantize_mx(out=out_words[:, a:b].bitcast(FP8X4), scales=out_scales[:, a:b], in_=tile[:])
+        for a, b in ((0, split), (split, 896), (896, U)):
             nc.sync.dma_start(words_hbm[:, a:b], out_words[:, a:b].bitcast(I32))
         for q in range(4):
             queue = nc.scalar if q % 2 else nc.sync

@@ -18,7 +18,7 @@ PACK = 4
 T, S, G, H, U = 1024, 512, 2048, 512, 1024
 K = 512
 CHUNK = 256
-SCALAR_GATHERS = (0, 2)
+SCALAR_GATHERS = (0, 768)
 FLOPS = 2 * 2 * K * H * S
 
 
@@ -139,12 +139,16 @@ def tile_picked_codegatepage_none_po_kernel(
             gained = keep.tile([P, PACK, CHUNK], F32, name=f"gained{c}")
             for t in range(PACK):
                 nc.scalar.activation(gained[:, t, :], h_banks[t][:, cols], ACT.Copy, scale=gains_16[:, t : t + 1])
-            offsets = n1_list[:, c * CHUNK // 16 : (c + 1) * CHUNK // 16]
             for t in range(PACK):
-                if t < SCALAR_GATHERS[c]:
-                    nc.scalar.activation(gates[:, t, :], sig_rows[t][:].indirect(offsets), ACT.Copy)
-                else:
-                    nc.vector.tensor_copy(gates[:, t, :], sig_rows[t][:].indirect(offsets))
+                on_scalar = min(max(SCALAR_GATHERS[c] - t * CHUNK, 0), CHUNK)
+                for start, stop in ((0, on_scalar), (on_scalar, CHUNK)):
+                    if start == stop:
+                        continue
+                    offsets = n1_list[:, (c * CHUNK + start) // 16 : (c * CHUNK + stop) // 16]
+                    if stop == on_scalar:
+                        nc.scalar.activation(gates[:, t, start:stop], sig_rows[t][:].indirect(offsets), ACT.Copy)
+                    else:
+                        nc.vector.tensor_copy(gates[:, t, start:stop], sig_rows[t][:].indirect(offsets))
             z = keep.tile([P, CHUNK * PACK], BF16, name=f"z{c}", align_bytes=64)
             nc.vector.tensor_tensor(
                 z[:].rearrange("p (b i t) -> p b t i", t=PACK, i=4),

@@ -135,7 +135,7 @@ def tile_picked_codegatepage_none_po_kernel(
         h2 = keep.tile([P, PACK, S], F32, name="h2")
         for c in range(S // CHUNK):
             cols = slice(c * CHUNK, (c + 1) * CHUNK)
-            gates = keep.tile([P, PACK, CHUNK], F32, name=f"gates{c}")
+            gates = keep.tile([P, PACK, CHUNK], F32, name=f"gates{c}", tag=f"gates{c}")
             gained = keep.tile([P, PACK, CHUNK], F32, name=f"gained{c}")
             for t in range(PACK):
                 nc.scalar.activation(gained[:, t, :], h_banks[t][:, cols], ACT.Copy, scale=gains_16[:, t : t + 1])
@@ -150,13 +150,17 @@ def tile_picked_codegatepage_none_po_kernel(
                     else:
                         nc.vector.tensor_copy(gates[:, t, start:stop], sig_rows[t][:].indirect(offsets))
             z = keep.tile([P, CHUNK * PACK], BF16, name=f"z{c}", align_bytes=64)
-            nc.vector.tensor_tensor(
+            engine = nc.gpsimd if c else nc.vector
+            engine.tensor_tensor(
                 z[:].rearrange("p (b i t) -> p b t i", t=PACK, i=4),
                 gained[:].rearrange("p t (b i) -> p b t i", i=4),
                 gates[:].rearrange("p t (b i) -> p b t i", i=4),
                 MULT,
             )
-            z_words = keep.tile([P, CHUNK], U32, name=f"z_words{c}", align_bytes=64)
+            if c:
+                h2_held = keep.tile([P, CHUNK], F32, name="h2_held", tag=f"gates{c}")
+                nc.scalar.activation(h2_held[:], held_bank[:, 0, :], ACT.Copy, scale=0.0625)
+            z_words = keep.tile([P, CHUNK], U32, name=f"z_words{c}", tag=f"z_words{c}", align_bytes=64)
             z_scales = keep.tile([P, CHUNK], U8, name=f"z_scales{c}", align_bytes=64)
             nc.vector.quantize_mx(out=z_words[:].bitcast(FP8X4), scales=z_scales[:], in_=z[:])
             for pair in range(2):
@@ -173,16 +177,25 @@ def tile_picked_codegatepage_none_po_kernel(
                         start=True,
                         stop=True,
                     )
-                nc.scalar.activation(h2[:, 2 * pair : 2 * pair + 2, cols], h2_bank[:], ACT.Copy, scale=0.0625)
+                if c == 0 and pair == 1:
+                    held_bank = h2_bank
+                    nc.scalar.activation(h2[:, 3, cols], h2_bank[:, 1, :], ACT.Copy, scale=0.0625)
+                elif c == 0:
+                    h2_first = keep.tile([P, CHUNK], F32, name="h2_first", tag="z_words1", align_bytes=64)
+                    nc.scalar.activation(h2_first[:], h2_bank[:, 0, :], ACT.Copy, scale=0.0625)
+                    nc.scalar.activation(h2[:, 1, cols], h2_bank[:, 1, :], ACT.Copy, scale=0.0625)
+                    nc.vector.tensor_copy(page[0][:].indirect(n2_list[:, 0 : CHUNK // 16]), h2_first[:])
+                    nc.vector.tensor_copy(page[1][:].indirect(n2_list[:, 0 : CHUNK // 16]), h2[:, 1, cols])
+                else:
+                    nc.scalar.activation(h2[:, 2 * pair : 2 * pair + 2, cols], h2_bank[:], ACT.Copy, scale=0.0625)
 
         def scatter(t, start, stop):
             nc.vector.tensor_copy(page[t][:].indirect(n2_list[:, start // 16 : stop // 16]), h2[:, t, start:stop])
 
-        for start in (0, CHUNK):
-            for t in range(2):
-                scatter(t, start, start + CHUNK)
-        for t in range(2, PACK):
-            scatter(t, 0, S)
+        nc.vector.tensor_copy(page[2][:].indirect(n2_list[:, 0 : CHUNK // 16]), h2_held[:])
+        for t in range(3):
+            scatter(t, CHUNK, S)
+        scatter(3, 0, S)
 
         for t in range(PACK):
             nc.sync.dma_start(out_rows[:, t, :], page[t][:])

from contextlib import ExitStack

import concourse.mybir as mybir

F32 = mybir.dt.float32
BF16 = mybir.dt.bfloat16
I32 = mybir.dt.int32
U32 = mybir.dt.uint32
U16 = mybir.dt.uint16
U8 = mybir.dt.uint8
FP8X4 = mybir.dt.float8_e4m3fn_x4
ACT = mybir.ActivationFunctionType
MULT = mybir.AluOpType.mult
ADD = mybir.AluOpType.add

P = 128
PACK = 4
T, S, G, H, U = 1024, 512, 2048, 512, 1024
K = 512
CHUNK = 256
SCALAR_GATHERS = (0, 768)
FLOPS = 2 * 2 * K * H * S


def tile_picked_codegatepage_none_po_kernel(
    tc, x_words, x_scales, d_words, d_scales, gs, mem, offs, k1, n1, k2, n2, out_0, out_1, out_2
):
    nc = tc.nc
    with ExitStack() as ctx:
        lists = ctx.enter_context(tc.tile_pool(name="lists", bufs=1))
        keep = ctx.enter_context(tc.tile_pool(name="keep", bufs=1))
        pages = ctx.enter_context(tc.tile_pool(name="pages", bufs=1))
        picks = ctx.enter_context(tc.tile_pool(name="picks", bufs=1))
        psum = ctx.enter_context(tc.psum_pool(name="psum", bufs=1))

        def load_list(name, source):
            tile = lists.tile([P, S // 16], U16, name=name)
            nc.sync.dma_start(tile[:], source)
            return tile

        def load_scale_rows(name, source, width):
            tile = keep.tile([P, width], U8, name=name, align_bytes=64)
            rows = source[0].bitcast(I32).unsqueeze(1).to_broadcast([16, 8, width // 4])
            nc.sync.dma_start(tile[:].bitcast(I32), rows)
            return tile

        def load_words(name, source, width):
            tile = keep.tile([P, width], U32, name=name, align_bytes=64)
            nc.sync.dma_start(tile[:].bitcast(I32), source[0].rearrange("p c r -> p (c r)").bitcast(I32))
            return tile

        offs_list = load_list("offs_list", offs)
        x_scale_table = load_scale_rows("x_scale_table", x_scales, T)
        k1_list = load_list("k1_list", k1)
        d_scale_table = load_scale_rows("d_scale_table", d_scales, G)
        d_word_table = load_words("d_word_table", d_words, G)
        x_word_table = load_words("x_word_table", x_words, T)
        k2_list = load_list("k2_list", k2)
        n1_list = load_list("n1_list", n1)
        gains = keep.tile([P, PACK], F32, name="gains")
        nc.gpsimd.dma_start(gains[:], gs.rearrange("(p t) o -> p (t o)", t=PACK))
        n2_list = load_list("n2_list", n2)

        plane_1 = keep.tile([P, H + S], U8, name="plane_1", align_bytes=64)
        plane_2 = keep.tile([P, H], U8, name="plane_2", align_bytes=64)
        nc.gpsimd.memset(plane_1[:].bitcast(I32), 0)
        nc.gpsimd.memset(plane_2[:].bitcast(I32), 0)

        def gather(name, table, index_list, dtype, offset=None):
            pool = keep if offset is None else picks
            tile = pool.tile([P, S], dtype, name=name, align_bytes=64, offset=offset)
            nc.vector.tensor_copy(tile[:], table[:].indirect(index_list[:]))
            return tile

        def deal(dealt, picked, run):
            nc.vector.tensor_copy(
                dealt.rearrange("p (t b i) -> p b t i", t=PACK, i=run),
                picked.rearrange("p (b i t) -> p b t i", t=PACK, i=run),
            )

        def place_scale_rows(plane, staged):
            for q in range(4):
                nc.sync.dma_start(
                    plane[32 * q : 32 * q + 4, :].bitcast(I32),
                    staged[32 * q : 32 * q + 32 : 8, :].bitcast(I32),
                )

        page_bytes = 4 * U
        staged_1 = pages.tile([P, H + S], U8, name="staged_1", offset=page_bytes - 512)
        staged_2 = pages.tile([P, H], U8, name="staged_2", offset=3 * page_bytes - 256)

        x_picked_scales = gather("x_picked_scales", x_scale_table, offs_list, U8)
        k1_scales = gather("k1_scales", d_scale_table, k1_list, U8)
        nc.vector.tensor_copy(staged_1[:, H : H + S].bitcast(I32), x_picked_scales[:].bitcast(I32))
        deal(staged_1[:, 0:H], k1_scales[:], 16)
        place_scale_rows(plane_1, staged_1)
        k1_words = gather("k1_words", d_word_table, k1_list, U32, 0)
        x_picked = gather("x_picked", x_word_table, offs_list, U32)
        w1 = keep.tile([P, H], U32, name="w1", align_bytes=64)
        deal(w1[:].bitcast(I32), k1_words[:].bitcast(I32), 4)

        gains_16 = keep.tile([P, PACK], F32, name="gains_16")
        nc.gpsimd.tensor_scalar(gains_16[:], gains[:], 0.0625, 0.0, MULT, ADD)

        h_banks = [psum.tile([P, S], F32, name=f"h_bank{t}") for t in range(PACK)]
        for t in range(PACK):
            rows = slice(P * t, P * (t + 1))
            nc.tensor.matmul_mx(
                out=h_banks[t][:],
                lhsT=w1[:, rows].bitcast(FP8X4),
                lhsT_scale=plane_1[:, rows],
                rhs=x_picked[:].bitcast(FP8X4),
                rhs_scale=plane_1[:, H : H + S],
                start=True,
                stop=True,
            )

        k2_scales = gather("k2_scales", d_scale_table, k2_list, U8, 0)
        deal(staged_2[:], k2_scales[:], 16)
        place_scale_rows(plane_2, staged_2)
        k2_words = gather("k2_words", d_word_table, k2_list, U32, S)
        w2 = keep.tile([P, H], U32, name="w2", align_bytes=64)
        deal(w2[:].bitcast(I32), k2_words[:].bitcast(I32), 4)

        page = [pages.tile([P, U], F32, name=f"page{t}", offset=page_bytes * t) for t in range(PACK)]
        mem_rows = mem.rearrange("(p t) w -> p t w", t=PACK)
        out_rows = out_0.rearrange("(p t) w -> p t w", t=PACK)
        for t in range(PACK):
            nc.sync.dma_start(page[t][:], mem_rows[:, t, :])

        sig_rows = [keep.tile([P, S], F32, name=f"sig_rows{t}") for t in range(PACK)]
        for t in range(PACK):
            nc.scalar.activation(sig_rows[t][:], h_banks[t][:], ACT.Sigmoid, scale=0.0625)

        h2 = keep.tile([P, PACK, S], F32, name="h2")
        for c in range(S // CHUNK):
            cols = slice(c * CHUNK, (c + 1) * CHUNK)
            gates = keep.tile([P, PACK, CHUNK], F32, name=f"gates{c}", tag=f"gates{c}")
            gained = keep.tile([P, PACK, CHUNK], F32, name=f"gained{c}")
            for t in range(PACK):
                nc.scalar.activation(gained[:, t, :], h_banks[t][:, cols], ACT.Copy, scale=gains_16[:, t : t + 1])
            for t in range(PACK):
                on_scalar = min(max(SCALAR_GATHERS[c] - t * CHUNK, 0), CHUNK)
                for start, stop in ((0, on_scalar), (on_scalar, CHUNK)):
                    if start == stop:
                        continue
                    offsets = n1_list[:, (c * CHUNK + start) // 16 : (c * CHUNK + stop) // 16]
                    if stop == on_scalar:
                        nc.scalar.activation(gates[:, t, start:stop], sig_rows[t][:].indirect(offsets), ACT.Copy)
                    else:
                        nc.vector.tensor_copy(gates[:, t, start:stop], sig_rows[t][:].indirect(offsets))
            z = keep.tile([P, CHUNK * PACK], BF16, name=f"z{c}", align_bytes=64)
            engine = nc.gpsimd if c else nc.vector
            engine.tensor_tensor(
                z[:].rearrange("p (b i t) -> p b t i", t=PACK, i=4),
                gained[:].rearrange("p t (b i) -> p b t i", i=4),
                gates[:].rearrange("p t (b i) -> p b t i", i=4),
                MULT,
            )
            if c:
                h2_held = keep.tile([P, CHUNK], F32, name="h2_held", tag=f"gates{c}")
                nc.scalar.activation(h2_held[:], held_bank[:, 0, :], ACT.Copy, scale=0.0625)
            z_words = keep.tile([P, CHUNK], U32, name=f"z_words{c}", tag=f"z_words{c}", align_bytes=64)
            z_scales = keep.tile([P, CHUNK], U8, name=f"z_scales{c}", align_bytes=64)
            nc.vector.quantize_mx(out=z_words[:].bitcast(FP8X4), scales=z_scales[:], in_=z[:])
            for pair in range(2):
                h2_bank = psum.tile([P, 2, CHUNK], F32, name=f"h2_bank{c}_{pair}")
                for u in range(2):
                    t = 2 * pair + u
                    rows = slice(P * t, P * (t + 1))
                    nc.tensor.matmul_mx(
                        out=h2_bank[:, u, :],
                        lhsT=w2[:, rows].bitcast(FP8X4),
                        lhsT_scale=plane_2[:, rows],
                        rhs=z_words[:].bitcast(FP8X4),
                        rhs_scale=z_scales[:],
                        start=True,
                        stop=True,
                    )
                if c == 0 and pair == 1:
                    held_bank = h2_bank
                    nc.scalar.activation(h2[:, 3, cols], h2_bank[:, 1, :], ACT.Copy, scale=0.0625)
                elif c == 0:
                    h2_first = keep.tile([P, CHUNK], F32, name="h2_first", tag="z_words1", align_bytes=64)
                    nc.scalar.activation(h2_first[:], h2_bank[:, 0, :], ACT.Copy, scale=0.0625)
                    nc.scalar.activation(h2[:, 1, cols], h2_bank[:, 1, :], ACT.Copy, scale=0.0625)
                    nc.vector.tensor_copy(page[0][:].indirect(n2_list[:, 0 : CHUNK // 16]), h2_first[:])
                    nc.vector.tensor_copy(page[1][:].indirect(n2_list[:, 0 : CHUNK // 16]), h2[:, 1, cols])
                else:
                    nc.scalar.activation(h2[:, 2 * pair : 2 * pair + 2, cols], h2_bank[:], ACT.Copy, scale=0.0625)

        def scatter(t, start, stop):
            nc.vector.tensor_copy(page[t][:].indirect(n2_list[:, start // 16 : stop // 16]), h2[:, t, start:stop])

        nc.vector.tensor_copy(page[2][:].indirect(n2_list[:, 0 : CHUNK // 16]), h2_held[:])
        for t in range(3):
            scatter(t, CHUNK, S)
        scatter(3, 0, S)

        for t in range(PACK):
            nc.sync.dma_start(out_rows[:, t, :], page[t][:])

        split = 384
        rounded = keep.tile([P, PACK, U], BF16, name="rounded")
        for t in range(PACK - 2):
            nc.scalar.copy(rounded[:, t, :], page[t][:])
        nc.scalar.copy(rounded[:, PACK - 2, split:U], page[PACK - 2][:, split:U])
        nc.scalar.copy(rounded[:, PACK - 2, 0:split], page[PACK - 2][:, 0:split])
        vector_pieces = [(0, 128), (128, split)]
        scalar_pieces = [(split, 640), (640, 896), (896, U)]
        pieces = vector_pieces + scalar_pieces
        grouped = [keep.tile([P, (b - a) * PACK], BF16, name=f"grouped{a}", align_bytes=64) for a, b in pieces]
        for (a, b), tile in zip(scalar_pieces, grouped[2:]):
            nc.scalar.copy(
                tile[:].rearrange("p (b i t) -> p b t i", t=PACK, i=4)[:, :, 0 : PACK - 1, :],
                rounded[:, 0 : PACK - 1, a:b].rearrange("p t (b i) -> p b t i", i=4),
            )
        for (a, b), tile in zip(scalar_pieces, grouped[2:]):
            nc.scalar.copy(tile[:].rearrange("p (c t) -> p c t", t=PACK)[:, :, PACK - 1], page[PACK - 1][:, a:b])
        for a, b in vector_pieces:
            nc.vector.tensor_copy(rounded[:, PACK - 1, a:b], page[PACK - 1][:, a:b])
        for (a, b), tile in zip(vector_pieces, grouped):
            nc.vector.tensor_copy(
                tile[:].rearrange("p (b i t) -> p b t i", t=PACK, i=4),
                rounded[:, :, a:b].rearrange("p t (b i) -> p b t i", i=4),
            )
        out_words = keep.tile([P, U], U32, name="out_words", align_bytes=64)
        out_scales = keep.tile([P, U], U8, name="out_scales", align_bytes=64)
        words_hbm = out_1[0].rearrange("p c r -> p (c r)").bitcast(I32)
        scales_hbm = out_2[0].bitcast(I32)
        for (a, b), tile in zip(pieces, grouped):
            nc.vector.quantize_mx(out=out_words[:, a:b].bitcast(FP8X4), scales=out_scales[:, a:b], in_=tile[:])
        for a, b in ((0, split), (split, 896), (896, U)):
            nc.sync.dma_start(words_hbm[:, a:b], out_words[:, a:b].bitcast(I32))
        for q in range(4):
            queue = nc.scalar if q % 2 else nc.sync
            queue.dma_start(scales_hbm[4 * q : 4 * q + 4, :], out_scales[32 * q : 32 * q + 4, :].bitcast(I32))
